import numpy as np
import ml_dtypes


def mxq(x, axis, fmt="e4m3"):
    dtype, down = {"e4m3": (ml_dtypes.float8_e4m3fn, 7), "e5m2": (ml_dtypes.float8_e5m2, 14)}[fmt]
    v = np.moveaxis(np.asarray(x, np.float32).astype(ml_dtypes.bfloat16).astype(np.float64), axis, -1)
    blocks = v.reshape(v.shape[:-1] + (-1, 32))
    amax = np.abs(blocks).max(-1, keepdims=True)
    byte = np.maximum(np.where(amax > 0, np.frexp(amax)[1] - 1 + 127, 0) - down, 1)
    scale = np.exp2(byte - 127.0)
    codes = (blocks / scale).astype(np.float32).astype(dtype).astype(np.float64)
    return np.moveaxis((codes * scale).reshape(v.shape), -1, axis)


WIDE = False


def mx_kscale(k):
    if not WIDE:
        return np.ones(k)
    levels = np.array([10, -10, 5, -5, 0])
    if k % 512:
        return np.exp2(np.random.permutation(np.resize(levels, k // 32))).repeat(32)
    a = np.empty((k // 512, 16))
    for p in range(k // 512):
        a[p, :8] = np.random.permutation(np.resize(levels, 8))
        for g in range(8):
            far = levels[np.abs(levels - a[p, g]) >= 10]
            a[p, g + 8] = far[np.random.randint(len(far))]
    return np.exp2(a.ravel()).repeat(32)


def f64(x):
    return np.asarray(x).astype(np.float64)


def striped(idx):
    return np.tile(idx.reshape(-1, 16).T, (8, 1)).astype(np.uint16)


def unstriped(offs):
    return offs[:16].T.reshape(-1).astype(np.int64)


def striped8(idx):
    return np.concatenate([x.reshape(-1, 16).T for x in idx]).astype(np.uint16)


def runs(offs, k):
    lists = np.stack([offs[16 * r : 16 * r + 16].T.reshape(-1) for r in range(8)]).astype(np.int64)
    return lists[np.arange(k) % 512 // 64]


def pack_weight(w):
    k, n = w.shape
    w = f64(np.asarray(w, np.float32).astype(ml_dtypes.bfloat16)).reshape(k // 32, 32, n)
    amax = np.abs(w).max(1)
    byte = np.clip(np.where(amax > 0, np.frexp(amax)[1] - 1 + 127 - 7, 1), 1, 254)
    scaled = (w * np.exp2(127.0 - byte)[:, None, :]).reshape(k, n).astype(np.float32)
    words = np.ascontiguousarray(scaled.reshape(k // 512, 128, 4, n).transpose(0, 1, 3, 2)).astype(ml_dtypes.float8_e4m3fn).view(np.uint8)
    return words, np.ascontiguousarray(byte.astype(np.uint8).reshape(k // 512, 16, n))


def unpack_weight(words, scales):
    g, p, n, _ = words.shape
    vals = np.ascontiguousarray(words).view(ml_dtypes.float8_e4m3fn).astype(np.float64) * np.repeat(np.exp2(scales.astype(np.float64) - 127.0), 8, axis=1)[..., None]
    return vals.transpose(0, 1, 3, 2).reshape(g * 512, n)


def sigmoid(v):
    return 1.0 / (1.0 + np.exp(-np.maximum(v, -700.0)))

def planes(y):
    n, m = y.shape
    v = y.astype(np.float32).astype(ml_dtypes.bfloat16).astype(np.float64).reshape(n // 32, 32, m)
    top = np.abs(v).max(1)
    byte = np.clip(np.where(top > 0, np.frexp(top)[1] - 1 + 127 - 7, 1), 1, 254)
    codes = (v * np.exp2(127.0 - byte)[:, None, :]).reshape(n, m).astype(np.float32).astype(ml_dtypes.float8_e4m3fn).view(np.uint8)
    words = codes.reshape(n // 512, 128, 4, m).transpose(0, 1, 3, 2)
    return np.ascontiguousarray(words), np.ascontiguousarray(byte.astype(np.uint8).reshape(n // 512, 16, m))


K, T, S, G, H, W = 512, 1024, 512, 2048, 512, 1024


def setup_inputs():
    n = np.random.standard_normal
    s = mx_kscale(K)[:, None]
    packed_xT = pack_weight(n((K, T)) * s)
    packed_dT = pack_weight(n((K, G)) / s)
    return {
        "x_words": packed_xT[0],
        "x_scales": packed_xT[1],
        "d_words": packed_dT[0],
        "d_scales": packed_dT[1],
        "gs": (np.random.uniform(0.5, 1.5, (K, 1)) * s).astype(np.float32),
        "sl": np.random.uniform(1.0, 2.0, (H, 1)).astype(np.float32),
        "th": (0.5 * n((H, 1))).astype(np.float32),
        "sl2": np.random.uniform(1.0, 2.0, (H, 1)).astype(np.float32),
        "th2": (0.5 * n((H, 1))).astype(np.float32),
        "offs": striped(np.random.permutation(T)[:S]),
        "k1": striped8(np.random.randint(0, G, (8, H))),
        "n1": striped(np.random.randint(0, S, W)),
        "n2": striped(np.random.permutation(S)),
        "k2": striped8(np.random.randint(0, G, (8, H))),
        "n3": striped8(np.stack([np.random.permutation(S) for _ in range(8)])),
        "n4": striped8(np.stack([np.random.permutation(S) for _ in range(8)])),
    }


def reference(x_words, x_scales, d_words, d_scales, gs, sl, th, sl2, th2, offs, k1, n1, n2, k2, n3, n4):
    d_k2 = unpack_weight(d_words, d_scales)[np.arange(K)[:, None], runs(k2, K)]
    d_k1 = unpack_weight(d_words, d_scales)[np.arange(K)[:, None], runs(k1, K)]
    xq = unpack_weight(x_words, x_scales)[:, unstriped(offs)]
    h = 0.0625 * (d_k1.T @ xq)
    mb = h[:, unstriped(n1)]
    mx = mb.reshape(H, S, 2).max(axis=2)
    st = h - mx
    z = f64(gs) * (np.maximum(st, st[:, unstriped(n2)]))
    h2 = 0.0625 * ((d_k2.T @ mxq(z, 0, "e4m3")))
    sg = sigmoid(f64(sl) * (h2[np.arange(H)[:, None], runs(n3, H)] - f64(th)))
    sg2 = sigmoid(f64(sl2) * (f64(th2) - (h2[np.arange(H)[:, None], runs(n4, H)])))
    out_0 = 2.0 * ((h2 * sg) * sg2)
    return (out_0,) + planes(out_0)

@@ -1,0 +1,247 @@
+from contextlib import ExitStack
+
+import concourse.mybir as mybir
+
+K, T, S, G, H = 512, 1024, 512, 2048, 512
+FLOPS = 2 * 2 * K * H * S
+
+F32 = mybir.dt.float32
+BF16 = mybir.dt.bfloat16
+I32 = mybir.dt.int32
+U32 = mybir.dt.uint32
+U16 = mybir.dt.uint16
+U8 = mybir.dt.uint8
+FP8X4 = mybir.dt.float8_e4m3fn_x4
+ALU = mybir.AluOpType
+ACT = mybir.ActivationFunctionType
+
+P = 128
+PACK = 4
+STRIPE = 16
+PIECE = 256
+Z_CHUNKS = ((0, 256), (256, 512))
+OUT_CHUNKS = ((0, 256), (256, 384), (384, 512))
+ROW_HOMES = (0, 8, 16, 24)
+
+
+def entries(offsets, first, last):
+    return offsets[:, first // STRIPE : last // STRIPE]
+
+
+def tile_picked_codeghopmecr_none_po_kernel(
+    tc, x_words, x_scales, d_words, d_scales, gs, sl, th, sl2, th2, offs, k1, n1, n2, k2, n3, n4, out_0, out_1, out_2
+):
+    nc = tc.nc
+
+    with ExitStack() as ctx:
+        keep = ctx.enter_context(tc.tile_pool(name="keep", bufs=1))
+        psum = ctx.enter_context(tc.psum_pool(name="psum", bufs=1))
+
+        def sb(name, shape, dtype, tag=None):
+            return keep.tile(shape, dtype, name=name, tag=tag or name, align_bytes=64)
+
+        def load_list(name, source):
+            offsets = sb(name, list(source.shape), U16)
+            nc.sync.dma_start(offsets[:], source)
+            return offsets
+
+        def load_rows(name, source):
+            rows = sb(name, [P, PACK], F32)
+            nc.gpsimd.dma_start(rows[:], source.rearrange("(p t) o -> p (t o)", t=PACK))
+            return rows
+
+        def load_scale_table(table, source):
+            rows = source[0].bitcast(I32)
+            nc.scalar.dma_start(table[:].bitcast(I32), rows.unsqueeze(1).to_broadcast([16, 8, rows.shape[1]]))
+
+        def place_scale_rows(placed, picked, queues):
+            for a, home in enumerate(ROW_HOMES):
+                queues[a % len(queues)].dma_start(
+                    placed[:].bitcast(I32)[a:P:32, :], picked[:].bitcast(I32)[home:P:32, :]
+                )
+
+        def deal(dealt, plain):
+            nc.vector.tensor_copy(
+                dealt.rearrange("p (t m) -> p t m", t=PACK), plain.rearrange("p (m t) -> p t m", t=PACK)
+            )
+
+        def gather(on_vector, out, window, offsets):
+            if on_vector:
+                nc.vector.tensor_copy(out, window[:].indirect(offsets))
+            else:
+                nc.scalar.activation(out, window[:].indirect(offsets), ACT.Copy)
+
+        def empty_bank(on_vector, out, bank):
+            if on_vector:
+                nc.vector.tensor_scalar(out, bank, 0.0625, None, ALU.mult)
+            else:
+                nc.scalar.activation(out, bank, ACT.Copy, scale=0.0625)
+
+        def interleave(grouped, planes):
+            nc.vector.tensor_copy(
+                grouped.rearrange("p (c i t) -> p c t i", i=4, t=PACK),
+                planes.rearrange("p t (c i) -> p c t i", i=4),
+            )
+
+        d_byte_table = sb("d_byte_table", [P, G], U8)
+        x_byte_table = sb("x_byte_table", [P, T], U8)
+        placed1 = sb("placed1", [P, H + S], U8)
+        placed2 = sb("placed2", [P, H], U8)
+        for zeroed in (placed1, placed2):
+            nc.vector.memset(zeroed[:].bitcast(I32), 0)
+
+        k1_list = load_list("k1_list", k1)
+        offs_list = load_list("offs_list", offs)
+        load_scale_table(d_byte_table, d_scales)
+        load_scale_table(x_byte_table, x_scales)
+        x_word_table = sb("x_word_table", [P, T], I32)
+        d_word_table = sb("d_word_table", [P, G], I32)
+        nc.sync.dma_start(x_word_table[:], x_words[0].rearrange("p n t -> p (n t)").bitcast(I32))
+        nc.sync.dma_start(d_word_table[:], d_words[0].rearrange("p n t -> p (n t)").bitcast(I32))
+        k2_list = load_list("k2_list", k2)
+        n1_list = load_list("n1_list", n1)
+        n2_list = load_list("n2_list", n2)
+        n3_list = load_list("n3_list", n3)
+        n4_list = load_list("n4_list", n4)
+        gs_rows = load_rows("gs_rows", gs)
+        sl_rows = load_rows("sl_rows", sl)
+        th_rows = load_rows("th_rows", th)
+        sl2_rows = load_rows("sl2_rows", sl2)
+        th2_rows = load_rows("th2_rows", th2)
+
+        picked1 = sb("picked1", [P, H + S], U8)
+        nc.vector.tensor_copy(picked1[:, 0:H], d_byte_table[:].indirect(k1_list[:]))
+        nc.vector.tensor_copy(picked1[:, H : H + S], x_byte_table[:].indirect(offs_list[:]))
+        place_scale_rows(placed1, picked1, (nc.scalar, nc.sync))
+
+        x_picked = sb("x_picked", [P, S], U32)
+        w1_picked = sb("w1_picked", [P, H], U32)
+        w1_words = sb("w1_words", [P, H], U32)
+        w1_bytes = sb("w1_bytes", [P, H], U8)
+        nc.vector.tensor_copy(x_picked[:], x_word_table[:].bitcast(U32).indirect(offs_list[:]))
+        nc.vector.tensor_copy(w1_picked[:], d_word_table[:].bitcast(U32).indirect(k1_list[:]))
+        deal(w1_words[:], w1_picked[:])
+        deal(w1_bytes[:], placed1[:, 0:H])
+
+        h = [sb(f"h{t}", [P, S], F32) for t in range(PACK)]
+        for t in range(PACK):
+            bank = psum.tile([P, S], F32, name=f"first{t}", tag=f"bank{t}")
+            cols = slice(t * P, (t + 1) * P)
+            nc.tensor.matmul_mx(
+                bank[:],
+                lhsT=w1_words[:, cols].bitcast(FP8X4),
+                lhsT_scale=w1_bytes[:, cols],
+                rhs=x_picked[:].bitcast(FP8X4),
+                rhs_scale=placed1[:, H : H + S],
+                start=True,
+                stop=True,
+            )
+            empty_bank(t > 0, h[t][:], bank[:])
+
+        bias1 = sb("bias1", [P, PACK], F32)
+        minus_sl = sb("minus_sl", [P, PACK], F32)
+        scale2 = sb("scale2", [P, PACK], F32)
+        bias2 = sb("bias2", [P, PACK], F32)
+        nc.gpsimd.tensor_scalar(minus_sl[:], sl_rows[:], -1.0, None, ALU.mult)
+        nc.gpsimd.tensor_tensor(bias1[:], minus_sl[:], th_rows[:], ALU.mult)
+        nc.gpsimd.tensor_scalar(scale2[:], sl2_rows[:], -1.0, None, ALU.mult)
+        nc.gpsimd.tensor_tensor(bias2[:], sl2_rows[:], th2_rows[:], ALU.mult)
+
+        picked2 = sb("picked2", [P, H], U8, tag="w1_bytes")
+        w2_picked = sb("w2_picked", [P, H], U32, tag="x_picked")
+        w2_words = sb("w2_words", [P, H], U32)
+        w2_bytes = sb("w2_bytes", [P, H], U8)
+        nc.vector.tensor_copy(picked2[:], d_byte_table[:].indirect(k2_list[:]))
+        place_scale_rows(placed2, picked2, (nc.sync,))
+        nc.vector.tensor_copy(w2_picked[:], d_word_table[:].bitcast(U32).indirect(k2_list[:]))
+        deal(w2_words[:], w2_picked[:])
+        deal(w2_bytes[:], placed2[:])
+
+        members = [sb(f"members{t}", [P, 2 * S], F32) for t in range(PACK)]
+        larger = [sb(f"larger{t}", [P, S], F32) for t in range(PACK)]
+        st = [sb(f"st{t}", [P, S], F32) for t in range(PACK)]
+        st_other = [sb(f"st_other{t}", [P, S], F32) for t in range(PACK)]
+        best = [sb(f"best{t}", [P, S], F32) for t in range(PACK)]
+        z_planes = sb("z_planes", [P, PACK, S], BF16)
+
+        def fetch_members(t):
+            for first in range(0, 2 * S, PIECE):
+                gather(False, members[t][:, first : first + PIECE], h[t], entries(n1_list, first, first + PIECE))
+
+        def make_st(t):
+            pairs = members[t][:].rearrange("p (j two) -> p j two", two=2)
+            nc.vector.tensor_tensor(larger[t][:], pairs[:, :, 0], pairs[:, :, 1], ALU.max)
+            nc.vector.tensor_tensor(st[t][:], h[t][:], larger[t][:], ALU.subtract)
+
+        def fetch_other(t):
+            for first in range(0, S, PIECE):
+                gather(t == 0, st_other[t][:, first : first + PIECE], st[t], entries(n2_list, first, first + PIECE))
+
+        def make_z(t):
+            nc.vector.tensor_tensor(best[t][:], st[t][:], st_other[t][:], ALU.max)
+            nc.vector.tensor_scalar(z_planes[:, t, :], best[t][:], gs_rows[:, t : t + 1], None, ALU.mult)
+
+        for t in range(PACK):
+            fetch_members(t)
+        make_st(0)
+        fetch_other(0)
+        make_z(0)
+        for t in range(1, PACK):
+            make_st(t)
+            fetch_other(t)
+        for t in range(1, PACK):
+            make_z(t)
+
+        h2 = [sb(f"h2_{t}", [P, S], F32) for t in range(PACK)]
+        for c, (first, last) in enumerate(Z_CHUNKS):
+            width = last - first
+            z_grouped = sb(f"z_grouped{c}", [P, PACK * width], BF16)
+            z_words = sb(f"z_words{c}", [P, width], U32)
+            z_bytes = sb(f"z_bytes{c}", [P, width], U8)
+            interleave(z_grouped[:], z_planes[:, :, first:last])
+            nc.vector.quantize_mx(z_words[:].bitcast(FP8X4), z_bytes[:], z_grouped[:])
+            for t in range(PACK):
+                bank = psum.tile([P, S], F32, name=f"second{c}_{t}", tag=f"bank{(PACK * (c + 1) + t) % 8}")
+                cols = slice(t * P, (t + 1) * P)
+                nc.tensor.matmul_mx(
+                    bank[:, 0:width],
+                    lhsT=w2_words[:, cols].bitcast(FP8X4),
+                    lhsT_scale=w2_bytes[:, cols],
+                    rhs=z_words[:].bitcast(FP8X4),
+                    rhs_scale=z_bytes[:],
+                    start=True,
+                    stop=True,
+                )
+                empty_bank(c > 0 and t > 0, h2[t][:, first:last], bank[:, 0:width])
+
+        out_rows = out_0.rearrange("(p t) s -> p t s", t=PACK)
+        out_words = out_1[0].rearrange("p n t -> p (n t)").bitcast(I32)
+        y_bytes = sb("y_bytes", [P, S], U8)
+        for c, (first, last) in enumerate(OUT_CHUNKS):
+            width = last - first
+            sg = sb(f"sg_{c}", [P, PACK, width], F32)
+            sg2 = sb(f"sg2_{c}", [P, PACK, width], F32)
+            gated = sb(f"gated{c}", [P, PACK, width], F32)
+            y = sb(f"y{c}", [P, PACK, width], F32)
+            for t in range(PACK):
+                one = slice(t, t + 1)
+                nc.scalar.activation(
+                    sg[:, t, :], h2[t][:].indirect(entries(n3_list, first, last)), ACT.Sigmoid,
+                    bias=bias1[:, one], scale=sl_rows[:, one],
+                )
+                nc.scalar.activation(
+                    sg2[:, t, :], h2[t][:].indirect(entries(n4_list, first, last)), ACT.Sigmoid,
+                    bias=bias2[:, one], scale=scale2[:, one],
+                )
+                nc.vector.scalar_tensor_tensor(gated[:, t, :], sg[:, t, :], 2.0, h2[t][:, first:last], ALU.mult, ALU.mult)
+                nc.vector.tensor_tensor(y[:, t, :], gated[:, t, :], sg2[:, t, :], ALU.mult)
+            nc.sync.dma_start(out_rows[:, :, first:last], y[:])
+            y_grouped = sb(f"y_grouped{c}", [P, PACK * width], BF16)
+            y_words = sb(f"y_words{c}", [P, width], I32)
+            interleave(y_grouped[:], y[:])
+            nc.vector.quantize_mx(y_words[:].bitcast(FP8X4), y_bytes[:, first:last], y_grouped[:])
+            nc.sync.dma_start(out_words[:, first:last], y_words[:])
+        out_bytes = out_2[0].bitcast(I32)
+        for q in range(4):
+            queue = nc.scalar if q % 2 else nc.sync
+            queue.dma_start(out_bytes[4 * q : 4 * q + 4, :], y_bytes[:].bitcast(I32)[32 * q : 32 * q + 4, :])

@@ -18,10 +18,9 @@ ACT = mybir.ActivationFunctionType
 P = 128
 PACK = 4
 STRIPE = 16
-PIECE = 256
 Z_CHUNKS = ((0, 256), (256, 512))
-OUT_CHUNKS = ((0, 256), (256, 384), (384, 512))
-ROW_HOMES = (0, 8, 16, 24)
+VECTOR_SHARE = 160
+SCALAR_MEMBERS = 384
 
 
 def entries(offsets, first, last):
@@ -50,19 +49,27 @@ def tile_picked_codeghopmecr_none_po_kernel(
             nc.gpsimd.dma_start(rows[:], source.rearrange("(p t) o -> p (t o)", t=PACK))
             return rows
 
-        def load_scale_table(table, source):
+        def load_scale_table(queue, table, source):
             rows = source[0].bitcast(I32)
-            nc.scalar.dma_start(table[:].bitcast(I32), rows.unsqueeze(1).to_broadcast([16, 8, rows.shape[1]]))
-
-        def place_scale_rows(placed, picked, queues):
-            for a, home in enumerate(ROW_HOMES):
-                queues[a % len(queues)].dma_start(
-                    placed[:].bitcast(I32)[a:P:32, :], picked[:].bitcast(I32)[home:P:32, :]
+            for e in range(2):
+                queue.dma_start(
+                    table[:].bitcast(I32)[e:P:2, :],
+                    rows[e:16:2, :].unsqueeze(1).to_broadcast([8, 8, rows.shape[1]]),
                 )
+
+        def place_odd_runs(plane, queues):
+            words = plane[:].bitcast(I32)
+            for e in range(2):
+                queues[e].dma_start(words[2 + e : P : 32, :], words[STRIPE + e : P : 32, :])
 
         def deal(dealt, plain):
             nc.vector.tensor_copy(
                 dealt.rearrange("p (t m) -> p t m", t=PACK), plain.rearrange("p (m t) -> p t m", t=PACK)
+            )
+
+        def deal_words(dealt, plain):
+            nc.vector.tensor_copy(
+                dealt.rearrange("p (t m) -> p m t", t=PACK), plain.rearrange("p (m t) -> p m t", t=PACK)
             )
 
         def gather(on_vector, out, window, offsets):
@@ -77,25 +84,31 @@ def tile_picked_codeghopmecr_none_po_kernel(
             else:
                 nc.scalar.activation(out, bank, ACT.Copy, scale=0.0625)
 
-        def interleave(grouped, planes):
-            nc.vector.tensor_copy(
+        def interleave(on_vector, grouped, planes):
+            copy = nc.vector.tensor_copy if on_vector else nc.scalar.copy
+            copy(
                 grouped.rearrange("p (c i t) -> p c t i", i=4, t=PACK),
                 planes.rearrange("p t (c i) -> p c t i", i=4),
             )
 
         d_byte_table = sb("d_byte_table", [P, G], U8)
         x_byte_table = sb("x_byte_table", [P, T], U8)
-        placed1 = sb("placed1", [P, H + S], U8)
-        placed2 = sb("placed2", [P, H], U8)
-        for zeroed in (placed1, placed2):
-            nc.vector.memset(zeroed[:].bitcast(I32), 0)
+        h = [sb(f"h{t}", [P, 2 * S + STRIPE], F32) for t in range(PACK)]
+        st = [sb(f"st{t}", [P, S + STRIPE], F32) for t in range(PACK)]
+        for window in h + st:
+            nc.vector.memset(window[:, S:], 0.0)
 
-        k1_list = load_list("k1_list", k1)
-        offs_list = load_list("offs_list", offs)
-        load_scale_table(d_byte_table, d_scales)
-        load_scale_table(x_byte_table, x_scales)
+        warm_in = sb("warm_in", [P, 1], F32)
+        warm_out = sb("warm_out", [P, 1], F32)
+        nc.vector.memset(warm_in[:], 0.0)
+        nc.scalar.activation(warm_out[:], warm_in[:], ACT.Sigmoid)
+
         x_word_table = sb("x_word_table", [P, T], I32)
         d_word_table = sb("d_word_table", [P, G], I32)
+        offs_list = load_list("offs_list", offs)
+        load_scale_table(nc.scalar, x_byte_table, x_scales)
+        k1_list = load_list("k1_list", k1)
+        load_scale_table(nc.sync, d_byte_table, d_scales)
         nc.sync.dma_start(x_word_table[:], x_words[0].rearrange("p n t -> p (n t)").bitcast(I32))
         nc.sync.dma_start(d_word_table[:], d_words[0].rearrange("p n t -> p (n t)").bitcast(I32))
         k2_list = load_list("k2_list", k2)
@@ -109,34 +122,37 @@ def tile_picked_codeghopmecr_none_po_kernel(
         sl2_rows = load_rows("sl2_rows", sl2)
         th2_rows = load_rows("th2_rows", th2)
 
-        picked1 = sb("picked1", [P, H + S], U8)
-        nc.vector.tensor_copy(picked1[:, 0:H], d_byte_table[:].indirect(k1_list[:]))
-        nc.vector.tensor_copy(picked1[:, H : H + S], x_byte_table[:].indirect(offs_list[:]))
-        place_scale_rows(placed1, picked1, (nc.scalar, nc.sync))
-
+        bytes1_picked = sb("bytes1_picked", [P, H + S], U8)
+        bytes1 = sb("bytes1", [P, H + S], U8)
+        nc.vector.tensor_copy(bytes1_picked[:, H:], x_byte_table[:].indirect(offs_list[:]))
+        nc.vector.tensor_copy(bytes1_picked[:, 0:H], d_byte_table[:].indirect(k1_list[:]))
+        nc.vector.tensor_copy(bytes1[:, H:].bitcast(I32), bytes1_picked[:, H:].bitcast(I32))
+        deal(bytes1[:, 0:H], bytes1_picked[:, 0:H])
+        place_odd_runs(bytes1, (nc.sync, nc.scalar))
         x_picked = sb("x_picked", [P, S], U32)
         w1_picked = sb("w1_picked", [P, H], U32)
         w1_words = sb("w1_words", [P, H], U32)
-        w1_bytes = sb("w1_bytes", [P, H], U8)
         nc.vector.tensor_copy(x_picked[:], x_word_table[:].bitcast(U32).indirect(offs_list[:]))
         nc.vector.tensor_copy(w1_picked[:], d_word_table[:].bitcast(U32).indirect(k1_list[:]))
-        deal(w1_words[:], w1_picked[:])
-        deal(w1_bytes[:], placed1[:, 0:H])
+        deal_words(w1_words[:], w1_picked[:])
 
-        h = [sb(f"h{t}", [P, S], F32) for t in range(PACK)]
+        w2_picked = sb("w2_picked", [P, H], U32, tag="w1_picked")
+        w2_words = sb("w2_words", [P, H], U32)
+        nc.vector.tensor_copy(w2_picked[:], d_word_table[:].bitcast(U32).indirect(k2_list[:]))
+
         for t in range(PACK):
             bank = psum.tile([P, S], F32, name=f"first{t}", tag=f"bank{t}")
             cols = slice(t * P, (t + 1) * P)
             nc.tensor.matmul_mx(
                 bank[:],
                 lhsT=w1_words[:, cols].bitcast(FP8X4),
-                lhsT_scale=w1_bytes[:, cols],
+                lhsT_scale=bytes1[:, cols],
                 rhs=x_picked[:].bitcast(FP8X4),
-                rhs_scale=placed1[:, H : H + S],
+                rhs_scale=bytes1[:, H:],
                 start=True,
                 stop=True,
             )
-            empty_bank(t > 0, h[t][:], bank[:])
+            empty_bank(t > 0, h[t][:, 0:S], bank[:])
 
         bias1 = sb("bias1", [P, PACK], F32)
         minus_sl = sb("minus_sl", [P, PACK], F32)
@@ -147,101 +163,134 @@ def tile_picked_codeghopmecr_none_po_kernel(
         nc.gpsimd.tensor_scalar(scale2[:], sl2_rows[:], -1.0, None, ALU.mult)
         nc.gpsimd.tensor_tensor(bias2[:], sl2_rows[:], th2_rows[:], ALU.mult)
 
-        picked2 = sb("picked2", [P, H], U8, tag="w1_bytes")
-        w2_picked = sb("w2_picked", [P, H], U32, tag="x_picked")
-        w2_words = sb("w2_words", [P, H], U32)
-        w2_bytes = sb("w2_bytes", [P, H], U8)
-        nc.vector.tensor_copy(picked2[:], d_byte_table[:].indirect(k2_list[:]))
-        place_scale_rows(placed2, picked2, (nc.sync,))
-        nc.vector.tensor_copy(w2_picked[:], d_word_table[:].bitcast(U32).indirect(k2_list[:]))
-        deal(w2_words[:], w2_picked[:])
-        deal(w2_bytes[:], placed2[:])
-
         members = [sb(f"members{t}", [P, 2 * S], F32) for t in range(PACK)]
         larger = [sb(f"larger{t}", [P, S], F32) for t in range(PACK)]
-        st = [sb(f"st{t}", [P, S], F32) for t in range(PACK)]
         st_other = [sb(f"st_other{t}", [P, S], F32) for t in range(PACK)]
         best = [sb(f"best{t}", [P, S], F32) for t in range(PACK)]
         z_planes = sb("z_planes", [P, PACK, S], BF16)
 
-        def fetch_members(t):
-            for first in range(0, 2 * S, PIECE):
-                gather(False, members[t][:, first : first + PIECE], h[t], entries(n1_list, first, first + PIECE))
+        def fetch_members(t, on_vector, first, last):
+            gather(on_vector, members[t][:, first:last], h[t], entries(n1_list, first, last))
 
-        def make_st(t):
+        def pair_max(t):
             pairs = members[t][:].rearrange("p (j two) -> p j two", two=2)
             nc.vector.tensor_tensor(larger[t][:], pairs[:, :, 0], pairs[:, :, 1], ALU.max)
-            nc.vector.tensor_tensor(st[t][:], h[t][:], larger[t][:], ALU.subtract)
+
+        def subtract(t):
+            nc.vector.tensor_tensor(st[t][:, 0:S], h[t][:, 0:S], larger[t][:], ALU.subtract)
 
         def fetch_other(t):
-            for first in range(0, S, PIECE):
-                gather(t == 0, st_other[t][:, first : first + PIECE], st[t], entries(n2_list, first, first + PIECE))
+            gather(False, st_other[t][:], st[t], n2_list[:])
 
-        def make_z(t):
-            nc.vector.tensor_tensor(best[t][:], st[t][:], st_other[t][:], ALU.max)
-            nc.vector.tensor_scalar(z_planes[:, t, :], best[t][:], gs_rows[:, t : t + 1], None, ALU.mult)
+        def take_larger(t):
+            nc.vector.tensor_tensor(best[t][:], st[t][:, 0:S], st_other[t][:], ALU.max)
 
+        def weigh(t, on_vector):
+            if on_vector:
+                nc.vector.tensor_scalar(z_planes[:, t, :], best[t][:], gs_rows[:, t : t + 1], None, ALU.mult)
+            else:
+                nc.scalar.activation(z_planes[:, t, :], best[t][:], ACT.Copy, scale=gs_rows[:, t : t + 1])
+
+        for t in range(PACK - 1):
+            fetch_members(t, False, 0, 2 * S)
+        fetch_members(3, False, 0, SCALAR_MEMBERS)
+        deal_words(w2_words[:], w2_picked[:])
+        pair_max(0)
+        bytes2_picked = sb("bytes2_picked", [P, H], U8, tag="x_picked")
+        w2_bytes = sb("w2_bytes", [P, H], U8)
+        nc.vector.tensor_copy(bytes2_picked[:], d_byte_table[:].indirect(k2_list[:]))
+        deal(w2_bytes[:], bytes2_picked[:])
+        place_odd_runs(w2_bytes, (nc.sync, nc.sync))
+        subtract(0)
+        pair_max(1)
+        fetch_members(3, True, SCALAR_MEMBERS, 2 * S)
+        subtract(1)
+        pair_max(2)
+        pair_max(3)
+        subtract(2)
+        subtract(3)
         for t in range(PACK):
-            fetch_members(t)
-        make_st(0)
-        fetch_other(0)
-        make_z(0)
-        for t in range(1, PACK):
-            make_st(t)
             fetch_other(t)
-        for t in range(1, PACK):
-            make_z(t)
+        take_larger(0)
+        take_larger(1)
+        weigh(0, True)
+        take_larger(2)
+        weigh(1, True)
+        weigh(2, False)
+        take_larger(3)
+        weigh(3, True)
 
-        h2 = [sb(f"h2_{t}", [P, S], F32) for t in range(PACK)]
+        h2 = h[0:3] + [sb("h2_3", [P, S], F32)]
+        z_words = []
+        z_bytes = []
         for c, (first, last) in enumerate(Z_CHUNKS):
             width = last - first
             z_grouped = sb(f"z_grouped{c}", [P, PACK * width], BF16)
-            z_words = sb(f"z_words{c}", [P, width], U32)
-            z_bytes = sb(f"z_bytes{c}", [P, width], U8)
-            interleave(z_grouped[:], z_planes[:, :, first:last])
-            nc.vector.quantize_mx(z_words[:].bitcast(FP8X4), z_bytes[:], z_grouped[:])
-            for t in range(PACK):
-                bank = psum.tile([P, S], F32, name=f"second{c}_{t}", tag=f"bank{(PACK * (c + 1) + t) % 8}")
-                cols = slice(t * P, (t + 1) * P)
-                nc.tensor.matmul_mx(
-                    bank[:, 0:width],
-                    lhsT=w2_words[:, cols].bitcast(FP8X4),
-                    lhsT_scale=w2_bytes[:, cols],
-                    rhs=z_words[:].bitcast(FP8X4),
-                    rhs_scale=z_bytes[:],
-                    start=True,
-                    stop=True,
-                )
-                empty_bank(c > 0 and t > 0, h2[t][:, first:last], bank[:, 0:width])
+            z_words.append(sb(f"z_words{c}", [P, width], U32))
+            z_bytes.append(sb(f"z_bytes{c}", [P, width], U8))
+            interleave(c == 0, z_grouped[:], z_planes[:, :, first:last])
+            nc.vector.quantize_mx(z_words[c][:].bitcast(FP8X4), z_bytes[c][:], z_grouped[:])
+
+        def second_product(t, c, bank):
+            first, last = Z_CHUNKS[c]
+            cols = slice(t * P, (t + 1) * P)
+            nc.tensor.matmul_mx(
+                bank[:, first:last],
+                lhsT=w2_words[:, cols].bitcast(FP8X4),
+                lhsT_scale=w2_bytes[:, cols],
+                rhs=z_words[c][:].bitcast(FP8X4),
+                rhs_scale=z_bytes[c][:],
+                start=True,
+                stop=True,
+            )
+
+        for c, (first, last) in enumerate(Z_CHUNKS):
+            bank = psum.tile([P, S], F32, name=f"second0_{c}", tag=f"bank{c}")
+            second_product(0, c, bank)
+            empty_bank(False, h2[0][:, first:last], bank[:, first:last])
+        for t in range(1, PACK):
+            bank = psum.tile([P, S], F32, name=f"second{t}", tag=f"bank{(t + 1) % 3}")
+            for c in range(len(Z_CHUNKS)):
+                second_product(t, c, bank)
+            empty_bank(True, h2[t][:, 0:S], bank[:])
 
         out_rows = out_0.rearrange("(p t) s -> p t s", t=PACK)
         out_words = out_1[0].rearrange("p n t -> p (n t)").bitcast(I32)
+        sg = sb("sg", [P, PACK, S], F32)
+        sg2 = sb("sg2", [P, PACK, S], F32)
+        gated = sb("gated", [P, PACK, S], F32)
+        y = sb("y", [P, PACK, S], F32)
         y_bytes = sb("y_bytes", [P, S], U8)
-        for c, (first, last) in enumerate(OUT_CHUNKS):
+
+        def gate(t, first, last):
+            one = slice(t, t + 1)
+            cols = slice(first, last)
+            nc.scalar.activation(
+                sg[:, t, cols], h2[t][:].indirect(entries(n3_list, first, last)), ACT.Sigmoid,
+                bias=bias1[:, one], scale=sl_rows[:, one],
+            )
+            nc.scalar.activation(
+                sg2[:, t, cols], h2[t][:].indirect(entries(n4_list, first, last)), ACT.Sigmoid,
+                bias=bias2[:, one], scale=scale2[:, one],
+            )
+            nc.vector.scalar_tensor_tensor(gated[:, t, cols], sg[:, t, cols], 2.0, h2[t][:, cols], ALU.mult, ALU.mult)
+            nc.vector.tensor_tensor(y[:, t, cols], gated[:, t, cols], sg2[:, t, cols], ALU.mult)
+            nc.sync.dma_start(out_rows[:, t, cols], y[:, t, cols])
+
+        for t in range(PACK - 1):
+            gate(t, 0, S)
+        for c, (first, last) in enumerate(Z_CHUNKS):
             width = last - first
-            sg = sb(f"sg_{c}", [P, PACK, width], F32)
-            sg2 = sb(f"sg2_{c}", [P, PACK, width], F32)
-            gated = sb(f"gated{c}", [P, PACK, width], F32)
-            y = sb(f"y{c}", [P, PACK, width], F32)
-            for t in range(PACK):
-                one = slice(t, t + 1)
-                nc.scalar.activation(
-                    sg[:, t, :], h2[t][:].indirect(entries(n3_list, first, last)), ACT.Sigmoid,
-                    bias=bias1[:, one], scale=sl_rows[:, one],
-                )
-                nc.scalar.activation(
-                    sg2[:, t, :], h2[t][:].indirect(entries(n4_list, first, last)), ACT.Sigmoid,
-                    bias=bias2[:, one], scale=scale2[:, one],
-                )
-                nc.vector.scalar_tensor_tensor(gated[:, t, :], sg[:, t, :], 2.0, h2[t][:, first:last], ALU.mult, ALU.mult)
-                nc.vector.tensor_tensor(y[:, t, :], gated[:, t, :], sg2[:, t, :], ALU.mult)
-            nc.sync.dma_start(out_rows[:, :, first:last], y[:])
+            gate(3, first, last)
             y_grouped = sb(f"y_grouped{c}", [P, PACK * width], BF16)
             y_words = sb(f"y_words{c}", [P, width], I32)
-            interleave(y_grouped[:], y[:])
+            shared = width if c == 0 else VECTOR_SHARE
+            interleave(True, y_grouped[:, 0 : PACK * shared], y[:, :, first : first + shared])
+            if shared < width:
+                interleave(False, y_grouped[:, PACK * shared :], y[:, :, first + shared : last])
             nc.vector.quantize_mx(y_words[:].bitcast(FP8X4), y_bytes[:, first:last], y_grouped[:])
             nc.sync.dma_start(out_words[:, first:last], y_words[:])
         out_bytes = out_2[0].bitcast(I32)
         for q in range(4):
-            queue = nc.scalar if q % 2 else nc.sync
+            queue = nc.sync if q % 2 else nc.scalar
             queue.dma_start(out_bytes[4 * q : 4 * q + 4, :], y_bytes[:].bitcast(I32)[32 * q : 32 * q + 4, :])

@@ -19,8 +19,8 @@ P = 128
 PACK = 4
 STRIPE = 16
 Z_CHUNKS = ((0, 256), (256, 512))
-VECTOR_SHARE = 160
-SCALAR_MEMBERS = 384
+VECTOR_SHARE = 168
+SCALAR_MEMBERS = 448
 
 
 def entries(offsets, first, last):
@@ -122,6 +122,15 @@ def tile_picked_codeghopmecr_none_po_kernel(
         sl2_rows = load_rows("sl2_rows", sl2)
         th2_rows = load_rows("th2_rows", th2)
 
+        bias1 = sb("bias1", [P, PACK], F32)
+        minus_sl = sb("minus_sl", [P, PACK], F32)
+        scale2 = sb("scale2", [P, PACK], F32)
+        bias2 = sb("bias2", [P, PACK], F32)
+        nc.gpsimd.tensor_scalar(minus_sl[:], sl_rows[:], -1.0, None, ALU.mult)
+        nc.gpsimd.tensor_tensor(bias1[:], minus_sl[:], th_rows[:], ALU.mult)
+        nc.gpsimd.tensor_scalar(scale2[:], sl2_rows[:], -1.0, None, ALU.mult)
+        nc.gpsimd.tensor_tensor(bias2[:], sl2_rows[:], th2_rows[:], ALU.mult)
+
         bytes1_picked = sb("bytes1_picked", [P, H + S], U8)
         bytes1 = sb("bytes1", [P, H + S], U8)
         nc.vector.tensor_copy(bytes1_picked[:, H:], x_byte_table[:].indirect(offs_list[:]))
@@ -140,28 +149,26 @@ def tile_picked_codeghopmecr_none_po_kernel(
         w2_words = sb("w2_words", [P, H], U32)
         nc.vector.tensor_copy(w2_picked[:], d_word_table[:].bitcast(U32).indirect(k2_list[:]))
 
-        for t in range(PACK):
-            bank = psum.tile([P, S], F32, name=f"first{t}", tag=f"bank{t}")
+        def first_product(t, first, last, bank):
             cols = slice(t * P, (t + 1) * P)
             nc.tensor.matmul_mx(
-                bank[:],
+                bank[:, first:last],
                 lhsT=w1_words[:, cols].bitcast(FP8X4),
                 lhsT_scale=bytes1[:, cols],
-                rhs=x_picked[:].bitcast(FP8X4),
-                rhs_scale=bytes1[:, H:],
+                rhs=x_picked[:, first:last].bitcast(FP8X4),
+                rhs_scale=bytes1[:, H + first : H + last],
                 start=True,
                 stop=True,
             )
-            empty_bank(t > 0, h[t][:, 0:S], bank[:])
 
-        bias1 = sb("bias1", [P, PACK], F32)
-        minus_sl = sb("minus_sl", [P, PACK], F32)
-        scale2 = sb("scale2", [P, PACK], F32)
-        bias2 = sb("bias2", [P, PACK], F32)
-        nc.gpsimd.tensor_scalar(minus_sl[:], sl_rows[:], -1.0, None, ALU.mult)
-        nc.gpsimd.tensor_tensor(bias1[:], minus_sl[:], th_rows[:], ALU.mult)
-        nc.gpsimd.tensor_scalar(scale2[:], sl2_rows[:], -1.0, None, ALU.mult)
-        nc.gpsimd.tensor_tensor(bias2[:], sl2_rows[:], th2_rows[:], ALU.mult)
+        for c, (first, last) in enumerate(Z_CHUNKS):
+            bank = psum.tile([P, S], F32, name=f"first0_{c}", tag=f"bank{4 * c}")
+            first_product(0, first, last, bank)
+            empty_bank(False, h[0][:, first:last], bank[:, first:last])
+        for t in range(1, PACK):
+            bank = psum.tile([P, S], F32, name=f"first{t}", tag=f"bank{t}")
+            first_product(t, 0, S, bank)
+            empty_bank(True, h[t][:, 0:S], bank[:])
 
         members = [sb(f"members{t}", [P, 2 * S], F32) for t in range(PACK)]
         larger = [sb(f"larger{t}", [P, S], F32) for t in range(PACK)]
@@ -179,17 +186,18 @@ def tile_picked_codeghopmecr_none_po_kernel(
         def subtract(t):
             nc.vector.tensor_tensor(st[t][:, 0:S], h[t][:, 0:S], larger[t][:], ALU.subtract)
 
-        def fetch_other(t):
-            gather(False, st_other[t][:], st[t], n2_list[:])
+        def fetch_other(t, first, last):
+            gather(False, st_other[t][:, first:last], st[t], entries(n2_list, first, last))
 
-        def take_larger(t):
-            nc.vector.tensor_tensor(best[t][:], st[t][:, 0:S], st_other[t][:], ALU.max)
+        def take_larger(t, first, last):
+            nc.vector.tensor_tensor(best[t][:, first:last], st[t][:, first:last], st_other[t][:, first:last], ALU.max)
 
-        def weigh(t, on_vector):
+        def weigh(t, on_vector, first, last):
+            out, in_, weight = z_planes[:, t, first:last], best[t][:, first:last], gs_rows[:, t : t + 1]
             if on_vector:
-                nc.vector.tensor_scalar(z_planes[:, t, :], best[t][:], gs_rows[:, t : t + 1], None, ALU.mult)
+                nc.vector.tensor_scalar(out, in_, weight, None, ALU.mult)
             else:
-                nc.scalar.activation(z_planes[:, t, :], best[t][:], ACT.Copy, scale=gs_rows[:, t : t + 1])
+                nc.scalar.activation(out, in_, ACT.Copy, scale=weight)
 
         for t in range(PACK - 1):
             fetch_members(t, False, 0, 2 * S)
@@ -209,18 +217,22 @@ def tile_picked_codeghopmecr_none_po_kernel(
         pair_max(3)
         subtract(2)
         subtract(3)
-        for t in range(PACK):
-            fetch_other(t)
-        take_larger(0)
-        take_larger(1)
-        weigh(0, True)
-        take_larger(2)
-        weigh(1, True)
-        weigh(2, False)
-        take_larger(3)
-        weigh(3, True)
+        for t in range(PACK - 1):
+            fetch_other(t, 0, S)
+        for first, last in reversed(Z_CHUNKS):
+            fetch_other(3, first, last)
+        take_larger(0, 0, S)
+        take_larger(1, 0, S)
+        weigh(0, True, 0, S)
+        take_larger(2, 0, S)
+        weigh(1, True, 0, S)
+        weigh(2, False, 0, S)
+        for first, last in reversed(Z_CHUNKS):
+            take_larger(3, first, last)
+        for first, last in reversed(Z_CHUNKS):
+            weigh(3, True, first, last)
 
-        h2 = h[0:3] + [sb("h2_3", [P, S], F32)]
+        h2 = members
         z_words = []
         z_bytes = []
         for c, (first, last) in enumerate(Z_CHUNKS):
@@ -249,7 +261,7 @@ def tile_picked_codeghopmecr_none_po_kernel(
             second_product(0, c, bank)
             empty_bank(False, h2[0][:, first:last], bank[:, first:last])
         for t in range(1, PACK):
-            bank = psum.tile([P, S], F32, name=f"second{t}", tag=f"bank{(t + 1) % 3}")
+            bank = psum.tile([P, S], F32, name=f"second{t}", tag=f"bank{1 + t % 2}")
             for c in range(len(Z_CHUNKS)):
                 second_product(t, c, bank)
             empty_bank(True, h2[t][:, 0:S], bank[:])
@@ -262,29 +274,32 @@ def tile_picked_codeghopmecr_none_po_kernel(
         y = sb("y", [P, PACK, S], F32)
         y_bytes = sb("y_bytes", [P, S], U8)
 
-        def gate(t, first, last):
+        def first_gate(t):
+            one = slice(t, t + 1)
+            nc.scalar.activation(
+                sg[:, t, :], h2[t][:].indirect(n3_list[:]), ACT.Sigmoid, bias=bias1[:, one], scale=sl_rows[:, one]
+            )
+            nc.vector.scalar_tensor_tensor(gated[:, t, :], sg[:, t, :], 2.0, h2[t][:, 0:S], ALU.mult, ALU.mult)
+
+        def second_gate(t, first, last):
             one = slice(t, t + 1)
             cols = slice(first, last)
-            nc.scalar.activation(
-                sg[:, t, cols], h2[t][:].indirect(entries(n3_list, first, last)), ACT.Sigmoid,
-                bias=bias1[:, one], scale=sl_rows[:, one],
-            )
             nc.scalar.activation(
                 sg2[:, t, cols], h2[t][:].indirect(entries(n4_list, first, last)), ACT.Sigmoid,
                 bias=bias2[:, one], scale=scale2[:, one],
             )
-            nc.vector.scalar_tensor_tensor(gated[:, t, cols], sg[:, t, cols], 2.0, h2[t][:, cols], ALU.mult, ALU.mult)
             nc.vector.tensor_tensor(y[:, t, cols], gated[:, t, cols], sg2[:, t, cols], ALU.mult)
-            nc.sync.dma_start(out_rows[:, t, cols], y[:, t, cols])
 
-        for t in range(PACK - 1):
-            gate(t, 0, S)
         for c, (first, last) in enumerate(Z_CHUNKS):
             width = last - first
-            gate(3, first, last)
+            for t in range(PACK):
+                if c == 0:
+                    first_gate(t)
+                second_gate(t, first, last)
+                nc.sync.dma_start(out_rows[:, t, first:last], y[:, t, first:last])
             y_grouped = sb(f"y_grouped{c}", [P, PACK * width], BF16)
             y_words = sb(f"y_words{c}", [P, width], I32)
-            shared = width if c == 0 else VECTOR_SHARE
+            shared = VECTOR_SHARE if last == S else width
             interleave(True, y_grouped[:, 0 : PACK * shared], y[:, :, first : first + shared])
             if shared < width:
                 interleave(False, y_grouped[:, PACK * shared :], y[:, :, first + shared : last])

@@ -17,14 +17,20 @@ ACT = mybir.ActivationFunctionType
 
 P = 128
 PACK = 4
-STRIPE = 16
-Z_CHUNKS = ((0, 256), (256, 512))
-VECTOR_SHARE = 168
-SCALAR_MEMBERS = 448
+LAST = PACK - 1
+GROUP = 16
+QUADRANT = 32
+SCALE_ROWS = 16
+RUNS = 8
+NEIGHBOURS = 4
+LAYER_FACTOR = 0.0625
+HALVES = ((0, S // 2), (S // 2, S))
+SCALAR_MEMBERS = 192
+VECTOR_COLUMNS = 168
 
 
 def entries(offsets, first, last):
-    return offsets[:, first // STRIPE : last // STRIPE]
+    return offsets[:, first // GROUP : last // GROUP]
 
 
 def tile_picked_codeghopmecr_none_po_kernel(
@@ -54,15 +60,15 @@ def tile_picked_codeghopmecr_none_po_kernel(
             for e in range(2):
                 queue.dma_start(
                     table[:].bitcast(I32)[e:P:2, :],
-                    rows[e:16:2, :].unsqueeze(1).to_broadcast([8, 8, rows.shape[1]]),
+                    rows[e:SCALE_ROWS:2, :].unsqueeze(1).to_broadcast([RUNS, GROUP // 2, rows.shape[1]]),
                 )
 
-        def place_odd_runs(plane, queues):
-            words = plane[:].bitcast(I32)
+        def place_odd_runs(scale_bytes):
+            as_int = scale_bytes[:].bitcast(I32)
             for e in range(2):
-                queues[e].dma_start(words[2 + e : P : 32, :], words[STRIPE + e : P : 32, :])
+                nc.sync.dma_start(as_int[2 + e : P : QUADRANT, :], as_int[GROUP + e : P : QUADRANT, :])
 
-        def deal(dealt, plain):
+        def deal_bytes(dealt, plain):
             nc.vector.tensor_copy(
                 dealt.rearrange("p (t m) -> p t m", t=PACK), plain.rearrange("p (m t) -> p t m", t=PACK)
             )
@@ -80,21 +86,21 @@ def tile_picked_codeghopmecr_none_po_kernel(
 
         def empty_bank(on_vector, out, bank):
             if on_vector:
-                nc.vector.tensor_scalar(out, bank, 0.0625, None, ALU.mult)
+                nc.vector.tensor_scalar(out, bank, LAYER_FACTOR, None, ALU.mult)
             else:
-                nc.scalar.activation(out, bank, ACT.Copy, scale=0.0625)
+                nc.scalar.activation(out, bank, ACT.Copy, scale=LAYER_FACTOR)
 
-        def interleave(on_vector, grouped, planes):
+        def interleave(on_vector, grouped, row_tiles):
             copy = nc.vector.tensor_copy if on_vector else nc.scalar.copy
             copy(
-                grouped.rearrange("p (c i t) -> p c t i", i=4, t=PACK),
-                planes.rearrange("p t (c i) -> p c t i", i=4),
+                grouped.rearrange("p (c i t) -> p c t i", i=NEIGHBOURS, t=PACK),
+                row_tiles.rearrange("p t (c i) -> p c t i", i=NEIGHBOURS),
             )
 
         d_byte_table = sb("d_byte_table", [P, G], U8)
         x_byte_table = sb("x_byte_table", [P, T], U8)
-        h = [sb(f"h{t}", [P, 2 * S + STRIPE], F32) for t in range(PACK)]
-        st = [sb(f"st{t}", [P, S + STRIPE], F32) for t in range(PACK)]
+        h = [sb(f"h{t}", [P, 2 * S + GROUP], F32) for t in range(PACK)]
+        st = [sb(f"st{t}", [P, S + GROUP], F32) for t in range(PACK)]
         for window in h + st:
             nc.vector.memset(window[:, S:], 0.0)
 
@@ -116,28 +122,30 @@ def tile_picked_codeghopmecr_none_po_kernel(
         n2_list = load_list("n2_list", n2)
         n3_list = load_list("n3_list", n3)
         n4_list = load_list("n4_list", n4)
-        gs_rows = load_rows("gs_rows", gs)
         sl_rows = load_rows("sl_rows", sl)
         th_rows = load_rows("th_rows", th)
         sl2_rows = load_rows("sl2_rows", sl2)
         th2_rows = load_rows("th2_rows", th2)
+        gs_rows = load_rows("gs_rows", gs)
 
-        bias1 = sb("bias1", [P, PACK], F32)
+        sg_bias = sb("sg_bias", [P, PACK], F32)
         minus_sl = sb("minus_sl", [P, PACK], F32)
-        scale2 = sb("scale2", [P, PACK], F32)
-        bias2 = sb("bias2", [P, PACK], F32)
-        nc.gpsimd.tensor_scalar(minus_sl[:], sl_rows[:], -1.0, None, ALU.mult)
-        nc.gpsimd.tensor_tensor(bias1[:], minus_sl[:], th_rows[:], ALU.mult)
-        nc.gpsimd.tensor_scalar(scale2[:], sl2_rows[:], -1.0, None, ALU.mult)
-        nc.gpsimd.tensor_tensor(bias2[:], sl2_rows[:], th2_rows[:], ALU.mult)
+        sg2_scale = sb("sg2_scale", [P, PACK], F32)
+        sg2_bias = sb("sg2_bias", [P, PACK], F32)
+        nc.scalar.activation(minus_sl[:], sl_rows[:], ACT.Copy, scale=-1.0)
+        nc.scalar.activation(sg2_scale[:], sl2_rows[:], ACT.Copy, scale=-1.0)
+        for t in range(PACK):
+            one = slice(t, t + 1)
+            nc.scalar.activation(sg_bias[:, one], th_rows[:, one], ACT.Copy, scale=minus_sl[:, one])
+            nc.scalar.activation(sg2_bias[:, one], th2_rows[:, one], ACT.Copy, scale=sl2_rows[:, one])
 
         bytes1_picked = sb("bytes1_picked", [P, H + S], U8)
         bytes1 = sb("bytes1", [P, H + S], U8)
         nc.vector.tensor_copy(bytes1_picked[:, H:], x_byte_table[:].indirect(offs_list[:]))
         nc.vector.tensor_copy(bytes1_picked[:, 0:H], d_byte_table[:].indirect(k1_list[:]))
         nc.vector.tensor_copy(bytes1[:, H:].bitcast(I32), bytes1_picked[:, H:].bitcast(I32))
-        deal(bytes1[:, 0:H], bytes1_picked[:, 0:H])
-        place_odd_runs(bytes1, (nc.sync, nc.scalar))
+        deal_bytes(bytes1[:, 0:H], bytes1_picked[:, 0:H])
+        place_odd_runs(bytes1)
         x_picked = sb("x_picked", [P, S], U32)
         w1_picked = sb("w1_picked", [P, H], U32)
         w1_words = sb("w1_words", [P, H], U32)
@@ -150,19 +158,19 @@ def tile_picked_codeghopmecr_none_po_kernel(
         nc.vector.tensor_copy(w2_picked[:], d_word_table[:].bitcast(U32).indirect(k2_list[:]))
 
         def first_product(t, first, last, bank):
-            cols = slice(t * P, (t + 1) * P)
+            features = slice(t * P, (t + 1) * P)
             nc.tensor.matmul_mx(
                 bank[:, first:last],
-                lhsT=w1_words[:, cols].bitcast(FP8X4),
-                lhsT_scale=bytes1[:, cols],
+                lhsT=w1_words[:, features].bitcast(FP8X4),
+                lhsT_scale=bytes1[:, features],
                 rhs=x_picked[:, first:last].bitcast(FP8X4),
                 rhs_scale=bytes1[:, H + first : H + last],
                 start=True,
                 stop=True,
             )
 
-        for c, (first, last) in enumerate(Z_CHUNKS):
-            bank = psum.tile([P, S], F32, name=f"first0_{c}", tag=f"bank{4 * c}")
+        for c, (first, last) in enumerate(HALVES):
+            bank = psum.tile([P, S], F32, name=f"first0_{c}", tag=f"bank{PACK * c}")
             first_product(0, first, last, bank)
             empty_bank(False, h[0][:, first:last], bank[:, first:last])
         for t in range(1, PACK):
@@ -174,7 +182,7 @@ def tile_picked_codeghopmecr_none_po_kernel(
         larger = [sb(f"larger{t}", [P, S], F32) for t in range(PACK)]
         st_other = [sb(f"st_other{t}", [P, S], F32) for t in range(PACK)]
         best = [sb(f"best{t}", [P, S], F32) for t in range(PACK)]
-        z_planes = sb("z_planes", [P, PACK, S], BF16)
+        z_tiles = sb("z_tiles", [P, PACK, S], BF16)
 
         def fetch_members(t, on_vector, first, last):
             gather(on_vector, members[t][:, first:last], h[t], entries(n1_list, first, last))
@@ -193,76 +201,76 @@ def tile_picked_codeghopmecr_none_po_kernel(
             nc.vector.tensor_tensor(best[t][:, first:last], st[t][:, first:last], st_other[t][:, first:last], ALU.max)
 
         def weigh(t, on_vector, first, last):
-            out, in_, weight = z_planes[:, t, first:last], best[t][:, first:last], gs_rows[:, t : t + 1]
+            out, in_, weight = z_tiles[:, t, first:last], best[t][:, first:last], gs_rows[:, t : t + 1]
             if on_vector:
                 nc.vector.tensor_scalar(out, in_, weight, None, ALU.mult)
             else:
                 nc.scalar.activation(out, in_, ACT.Copy, scale=weight)
 
-        for t in range(PACK - 1):
+        for t in range(LAST):
             fetch_members(t, False, 0, 2 * S)
-        fetch_members(3, False, 0, SCALAR_MEMBERS)
+        fetch_members(LAST, False, 0, SCALAR_MEMBERS)
         deal_words(w2_words[:], w2_picked[:])
         pair_max(0)
         bytes2_picked = sb("bytes2_picked", [P, H], U8, tag="x_picked")
         w2_bytes = sb("w2_bytes", [P, H], U8)
         nc.vector.tensor_copy(bytes2_picked[:], d_byte_table[:].indirect(k2_list[:]))
-        deal(w2_bytes[:], bytes2_picked[:])
-        place_odd_runs(w2_bytes, (nc.sync, nc.sync))
+        deal_bytes(w2_bytes[:], bytes2_picked[:])
+        place_odd_runs(w2_bytes)
         subtract(0)
         pair_max(1)
-        fetch_members(3, True, SCALAR_MEMBERS, 2 * S)
+        fetch_members(LAST, True, SCALAR_MEMBERS, 2 * S)
         subtract(1)
         pair_max(2)
-        pair_max(3)
+        pair_max(LAST)
         subtract(2)
-        subtract(3)
-        for t in range(PACK - 1):
+        subtract(LAST)
+        for t in range(LAST):
             fetch_other(t, 0, S)
-        for first, last in reversed(Z_CHUNKS):
-            fetch_other(3, first, last)
+        for first, last in reversed(HALVES):
+            fetch_other(LAST, first, last)
         take_larger(0, 0, S)
         take_larger(1, 0, S)
         weigh(0, True, 0, S)
         take_larger(2, 0, S)
         weigh(1, True, 0, S)
         weigh(2, False, 0, S)
-        for first, last in reversed(Z_CHUNKS):
-            take_larger(3, first, last)
-        for first, last in reversed(Z_CHUNKS):
-            weigh(3, True, first, last)
+        for first, last in reversed(HALVES):
+            take_larger(LAST, first, last)
+        for first, last in reversed(HALVES):
+            weigh(LAST, True, first, last)
 
         h2 = members
         z_words = []
         z_bytes = []
-        for c, (first, last) in enumerate(Z_CHUNKS):
+        for c, (first, last) in enumerate(HALVES):
             width = last - first
             z_grouped = sb(f"z_grouped{c}", [P, PACK * width], BF16)
             z_words.append(sb(f"z_words{c}", [P, width], U32))
             z_bytes.append(sb(f"z_bytes{c}", [P, width], U8))
-            interleave(c == 0, z_grouped[:], z_planes[:, :, first:last])
+            interleave(c == 0, z_grouped[:], z_tiles[:, :, first:last])
             nc.vector.quantize_mx(z_words[c][:].bitcast(FP8X4), z_bytes[c][:], z_grouped[:])
 
         def second_product(t, c, bank):
-            first, last = Z_CHUNKS[c]
-            cols = slice(t * P, (t + 1) * P)
+            first, last = HALVES[c]
+            features = slice(t * P, (t + 1) * P)
             nc.tensor.matmul_mx(
                 bank[:, first:last],
-                lhsT=w2_words[:, cols].bitcast(FP8X4),
-                lhsT_scale=w2_bytes[:, cols],
+                lhsT=w2_words[:, features].bitcast(FP8X4),
+                lhsT_scale=w2_bytes[:, features],
                 rhs=z_words[c][:].bitcast(FP8X4),
                 rhs_scale=z_bytes[c][:],
                 start=True,
                 stop=True,
             )
 
-        for c, (first, last) in enumerate(Z_CHUNKS):
+        for c, (first, last) in enumerate(HALVES):
             bank = psum.tile([P, S], F32, name=f"second0_{c}", tag=f"bank{c}")
             second_product(0, c, bank)
             empty_bank(False, h2[0][:, first:last], bank[:, first:last])
         for t in range(1, PACK):
             bank = psum.tile([P, S], F32, name=f"second{t}", tag=f"bank{1 + t % 2}")
-            for c in range(len(Z_CHUNKS)):
+            for c in range(len(HALVES)):
                 second_product(t, c, bank)
             empty_bank(True, h2[t][:, 0:S], bank[:])
 
@@ -277,7 +285,7 @@ def tile_picked_codeghopmecr_none_po_kernel(
         def first_gate(t):
             one = slice(t, t + 1)
             nc.scalar.activation(
-                sg[:, t, :], h2[t][:].indirect(n3_list[:]), ACT.Sigmoid, bias=bias1[:, one], scale=sl_rows[:, one]
+                sg[:, t, :], h2[t][:].indirect(n3_list[:]), ACT.Sigmoid, bias=sg_bias[:, one], scale=sl_rows[:, one]
             )
             nc.vector.scalar_tensor_tensor(gated[:, t, :], sg[:, t, :], 2.0, h2[t][:, 0:S], ALU.mult, ALU.mult)
 
@@ -286,11 +294,11 @@ def tile_picked_codeghopmecr_none_po_kernel(
             cols = slice(first, last)
             nc.scalar.activation(
                 sg2[:, t, cols], h2[t][:].indirect(entries(n4_list, first, last)), ACT.Sigmoid,
-                bias=bias2[:, one], scale=scale2[:, one],
+                bias=sg2_bias[:, one], scale=sg2_scale[:, one],
             )
             nc.vector.tensor_tensor(y[:, t, cols], gated[:, t, cols], sg2[:, t, cols], ALU.mult)
 
-        for c, (first, last) in enumerate(Z_CHUNKS):
+        for c, (first, last) in enumerate(HALVES):
             width = last - first
             for t in range(PACK):
                 if c == 0:
@@ -299,13 +307,15 @@ def tile_picked_codeghopmecr_none_po_kernel(
                 nc.sync.dma_start(out_rows[:, t, first:last], y[:, t, first:last])
             y_grouped = sb(f"y_grouped{c}", [P, PACK * width], BF16)
             y_words = sb(f"y_words{c}", [P, width], I32)
-            shared = VECTOR_SHARE if last == S else width
-            interleave(True, y_grouped[:, 0 : PACK * shared], y[:, :, first : first + shared])
-            if shared < width:
-                interleave(False, y_grouped[:, PACK * shared :], y[:, :, first + shared : last])
+            split = VECTOR_COLUMNS if last == S else width
+            interleave(True, y_grouped[:, 0 : PACK * split], y[:, :, first : first + split])
+            if split < width:
+                interleave(False, y_grouped[:, PACK * split :], y[:, :, first + split : last])
             nc.vector.quantize_mx(y_words[:].bitcast(FP8X4), y_bytes[:, first:last], y_grouped[:])
             nc.sync.dma_start(out_words[:, first:last], y_words[:])
         out_bytes = out_2[0].bitcast(I32)
-        for q in range(4):
+        for q in range(P // QUADRANT):
             queue = nc.sync if q % 2 else nc.scalar
-            queue.dma_start(out_bytes[4 * q : 4 * q + 4, :], y_bytes[:].bitcast(I32)[32 * q : 32 * q + 4, :])
+            queue.dma_start(
+                out_bytes[4 * q : 4 * q + 4, :], y_bytes[:].bitcast(I32)[QUADRANT * q : QUADRANT * q + 4, :]
+            )

from contextlib import ExitStack

import concourse.mybir as mybir

K, T, S, G, H = 512, 1024, 512, 2048, 512
FLOPS = 2 * 2 * K * H * S

F32 = mybir.dt.float32
BF16 = mybir.dt.bfloat16
I32 = mybir.dt.int32
U32 = mybir.dt.uint32
U16 = mybir.dt.uint16
U8 = mybir.dt.uint8
FP8X4 = mybir.dt.float8_e4m3fn_x4
ALU = mybir.AluOpType
ACT = mybir.ActivationFunctionType

P = 128
PACK = 4
LAST = PACK - 1
GROUP = 16
QUADRANT = 32
SCALE_ROWS = 16
RUNS = 8
NEIGHBOURS = 4
LAYER_FACTOR = 0.0625
HALVES = ((0, S // 2), (S // 2, S))
SCALAR_MEMBERS = 192
VECTOR_COLUMNS = 168


def entries(offsets, first, last):
    return offsets[:, first // GROUP : last // GROUP]


def tile_picked_codeghopmecr_none_po_kernel(
    tc, x_words, x_scales, d_words, d_scales, gs, sl, th, sl2, th2, offs, k1, n1, n2, k2, n3, n4, out_0, out_1, out_2
):
    nc = tc.nc

    with ExitStack() as ctx:
        keep = ctx.enter_context(tc.tile_pool(name="keep", bufs=1))
        psum = ctx.enter_context(tc.psum_pool(name="psum", bufs=1))

        def sb(name, shape, dtype, tag=None):
            return keep.tile(shape, dtype, name=name, tag=tag or name, align_bytes=64)

        def load_list(name, source):
            offsets = sb(name, list(source.shape), U16)
            nc.sync.dma_start(offsets[:], source)
            return offsets

        def load_rows(name, source):
            rows = sb(name, [P, PACK], F32)
            nc.gpsimd.dma_start(rows[:], source.rearrange("(p t) o -> p (t o)", t=PACK))
            return rows

        def load_scale_table(queue, table, source):
            rows = source[0].bitcast(I32)
            for e in range(2):
                queue.dma_start(
                    table[:].bitcast(I32)[e:P:2, :],
                    rows[e:SCALE_ROWS:2, :].unsqueeze(1).to_broadcast([RUNS, GROUP // 2, rows.shape[1]]),
                )

        def place_odd_runs(scale_bytes):
            as_int = scale_bytes[:].bitcast(I32)
            for e in range(2):
                nc.sync.dma_start(as_int[2 + e : P : QUADRANT, :], as_int[GROUP + e : P : QUADRANT, :])

        def deal_bytes(dealt, plain):
            nc.vector.tensor_copy(
                dealt.rearrange("p (t m) -> p t m", t=PACK), plain.rearrange("p (m t) -> p t m", t=PACK)
            )

        def deal_words(dealt, plain):
            nc.vector.tensor_copy(
                dealt.rearrange("p (t m) -> p m t", t=PACK), plain.rearrange("p (m t) -> p m t", t=PACK)
            )

        def gather(on_vector, out, window, offsets):
            if on_vector:
                nc.vector.tensor_copy(out, window[:].indirect(offsets))
            else:
                nc.scalar.activation(out, window[:].indirect(offsets), ACT.Copy)

        def empty_bank(on_vector, out, bank):
            if on_vector:
                nc.vector.tensor_scalar(out, bank, LAYER_FACTOR, None, ALU.mult)
            else:
                nc.scalar.activation(out, bank, ACT.Copy, scale=LAYER_FACTOR)

        def interleave(on_vector, grouped, row_tiles):
            copy = nc.vector.tensor_copy if on_vector else nc.scalar.copy
            copy(
                grouped.rearrange("p (c i t) -> p c t i", i=NEIGHBOURS, t=PACK),
                row_tiles.rearrange("p t (c i) -> p c t i", i=NEIGHBOURS),
            )

        d_byte_table = sb("d_byte_table", [P, G], U8)
        x_byte_table = sb("x_byte_table", [P, T], U8)
        h = [sb(f"h{t}", [P, 2 * S + GROUP], F32) for t in range(PACK)]
        st = [sb(f"st{t}", [P, S + GROUP], F32) for t in range(PACK)]
        for window in h + st:
            nc.vector.memset(window[:, S:], 0.0)

        warm_in = sb("warm_in", [P, 1], F32)
        warm_out = sb("warm_out", [P, 1], F32)
        nc.vector.memset(warm_in[:], 0.0)
        nc.scalar.activation(warm_out[:], warm_in[:], ACT.Sigmoid)

        x_word_table = sb("x_word_table", [P, T], I32)
        d_word_table = sb("d_word_table", [P, G], I32)
        offs_list = load_list("offs_list", offs)
        load_scale_table(nc.scalar, x_byte_table, x_scales)
        k1_list = load_list("k1_list", k1)
        load_scale_table(nc.sync, d_byte_table, d_scales)
        nc.sync.dma_start(x_word_table[:], x_words[0].rearrange("p n t -> p (n t)").bitcast(I32))
        nc.sync.dma_start(d_word_table[:], d_words[0].rearrange("p n t -> p (n t)").bitcast(I32))
        k2_list = load_list("k2_list", k2)
        n1_list = load_list("n1_list", n1)
        n2_list = load_list("n2_list", n2)
        n3_list = load_list("n3_list", n3)
        n4_list = load_list("n4_list", n4)
        sl_rows = load_rows("sl_rows", sl)
        th_rows = load_rows("th_rows", th)
        sl2_rows = load_rows("sl2_rows", sl2)
        th2_rows = load_rows("th2_rows", th2)
        gs_rows = load_rows("gs_rows", gs)

        sg_bias = sb("sg_bias", [P, PACK], F32)
        minus_sl = sb("minus_sl", [P, PACK], F32)
        sg2_scale = sb("sg2_scale", [P, PACK], F32)
        sg2_bias = sb("sg2_bias", [P, PACK], F32)
        nc.scalar.activation(minus_sl[:], sl_rows[:], ACT.Copy, scale=-1.0)
        nc.scalar.activation(sg2_scale[:], sl2_rows[:], ACT.Copy, scale=-1.0)
        for t in range(PACK):
            one = slice(t, t + 1)
            nc.scalar.activation(sg_bias[:, one], th_rows[:, one], ACT.Copy, scale=minus_sl[:, one])
            nc.scalar.activation(sg2_bias[:, one], th2_rows[:, one], ACT.Copy, scale=sl2_rows[:, one])

        bytes1_picked = sb("bytes1_picked", [P, H + S], U8)
        bytes1 = sb("bytes1", [P, H + S], U8)
        nc.vector.tensor_copy(bytes1_picked[:, H:], x_byte_table[:].indirect(offs_list[:]))
        nc.vector.tensor_copy(bytes1_picked[:, 0:H], d_byte_table[:].indirect(k1_list[:]))
        nc.vector.tensor_copy(bytes1[:, H:].bitcast(I32), bytes1_picked[:, H:].bitcast(I32))
        deal_bytes(bytes1[:, 0:H], bytes1_picked[:, 0:H])
        place_odd_runs(bytes1)
        x_picked = sb("x_picked", [P, S], U32)
        w1_picked = sb("w1_picked", [P, H], U32)
        w1_words = sb("w1_words", [P, H], U32)
        nc.vector.tensor_copy(x_picked[:], x_word_table[:].bitcast(U32).indirect(offs_list[:]))
        nc.vector.tensor_copy(w1_picked[:], d_word_table[:].bitcast(U32).indirect(k1_list[:]))
        deal_words(w1_words[:], w1_picked[:])

        w2_picked = sb("w2_picked", [P, H], U32, tag="w1_picked")
        w2_words = sb("w2_words", [P, H], U32)
        nc.vector.tensor_copy(w2_picked[:], d_word_table[:].bitcast(U32).indirect(k2_list[:]))

        def first_product(t, first, last, bank):
            features = slice(t * P, (t + 1) * P)
            nc.tensor.matmul_mx(
                bank[:, first:last],
                lhsT=w1_words[:, features].bitcast(FP8X4),
                lhsT_scale=bytes1[:, features],
                rhs=x_picked[:, first:last].bitcast(FP8X4),
                rhs_scale=bytes1[:, H + first : H + last],
                start=True,
                stop=True,
            )

        for c, (first, last) in enumerate(HALVES):
            bank = psum.tile([P, S], F32, name=f"first0_{c}", tag=f"bank{PACK * c}")
            first_product(0, first, last, bank)
            empty_bank(False, h[0][:, first:last], bank[:, first:last])
        for t in range(1, PACK):
            bank = psum.tile([P, S], F32, name=f"first{t}", tag=f"bank{t}")
            first_product(t, 0, S, bank)
            empty_bank(True, h[t][:, 0:S], bank[:])

        members = [sb(f"members{t}", [P, 2 * S], F32) for t in range(PACK)]
        larger = [sb(f"larger{t}", [P, S], F32) for t in range(PACK)]
        st_other = [sb(f"st_other{t}", [P, S], F32) for t in range(PACK)]
        best = [sb(f"best{t}", [P, S], F32) for t in range(PACK)]
        z_tiles = sb("z_tiles", [P, PACK, S], BF16)

        def fetch_members(t, on_vector, first, last):
            gather(on_vector, members[t][:, first:last], h[t], entries(n1_list, first, last))

        def pair_max(t):
            pairs = members[t][:].rearrange("p (j two) -> p j two", two=2)
            nc.vector.tensor_tensor(larger[t][:], pairs[:, :, 0], pairs[:, :, 1], ALU.max)

        def subtract(t):
            nc.vector.tensor_tensor(st[t][:, 0:S], h[t][:, 0:S], larger[t][:], ALU.subtract)

        def fetch_other(t, first, last):
            gather(False, st_other[t][:, first:last], st[t], entries(n2_list, first, last))

        def take_larger(t, first, last):
            nc.vector.tensor_tensor(best[t][:, first:last], st[t][:, first:last], st_other[t][:, first:last], ALU.max)

        def weigh(t, on_vector, first, last):
            out, in_, weight = z_tiles[:, t, first:last], best[t][:, first:last], gs_rows[:, t : t + 1]
            if on_vector:
                nc.vector.tensor_scalar(out, in_, weight, None, ALU.mult)
            else:
                nc.scalar.activation(out, in_, ACT.Copy, scale=weight)

        for t in range(LAST):
            fetch_members(t, False, 0, 2 * S)
        fetch_members(LAST, False, 0, SCALAR_MEMBERS)
        deal_words(w2_words[:], w2_picked[:])
        pair_max(0)
        bytes2_picked = sb("bytes2_picked", [P, H], U8, tag="x_picked")
        w2_bytes = sb("w2_bytes", [P, H], U8)
        nc.vector.tensor_copy(bytes2_picked[:], d_byte_table[:].indirect(k2_list[:]))
        deal_bytes(w2_bytes[:], bytes2_picked[:])
        place_odd_runs(w2_bytes)
        subtract(0)
        pair_max(1)
        fetch_members(LAST, True, SCALAR_MEMBERS, 2 * S)
        subtract(1)
        pair_max(2)
        pair_max(LAST)
        subtract(2)
        subtract(LAST)
        for t in range(LAST):
            fetch_other(t, 0, S)
        for first, last in reversed(HALVES):
            fetch_other(LAST, first, last)
        take_larger(0, 0, S)
        take_larger(1, 0, S)
        weigh(0, True, 0, S)
        take_larger(2, 0, S)
        weigh(1, True, 0, S)
        weigh(2, False, 0, S)
        for first, last in reversed(HALVES):
            take_larger(LAST, first, last)
        for first, last in reversed(HALVES):
            weigh(LAST, True, first, last)

        h2 = members
        z_words = []
        z_bytes = []
        for c, (first, last) in enumerate(HALVES):
            width = last - first
            z_grouped = sb(f"z_grouped{c}", [P, PACK * width], BF16)
            z_words.append(sb(f"z_words{c}", [P, width], U32))
            z_bytes.append(sb(f"z_bytes{c}", [P, width], U8))
            interleave(c == 0, z_grouped[:], z_tiles[:, :, first:last])
            nc.vector.quantize_mx(z_words[c][:].bitcast(FP8X4), z_bytes[c][:], z_grouped[:])

        def second_product(t, c, bank):
            first, last = HALVES[c]
            features = slice(t * P, (t + 1) * P)
            nc.tensor.matmul_mx(
                bank[:, first:last],
                lhsT=w2_words[:, features].bitcast(FP8X4),
                lhsT_scale=w2_bytes[:, features],
                rhs=z_words[c][:].bitcast(FP8X4),
                rhs_scale=z_bytes[c][:],
                start=True,
                stop=True,
            )

        for c, (first, last) in enumerate(HALVES):
            bank = psum.tile([P, S], F32, name=f"second0_{c}", tag=f"bank{c}")
            second_product(0, c, bank)
            empty_bank(False, h2[0][:, first:last], bank[:, first:last])
        for t in range(1, PACK):
            bank = psum.tile([P, S], F32, name=f"second{t}", tag=f"bank{1 + t % 2}")
            for c in range(len(HALVES)):
                second_product(t, c, bank)
            empty_bank(True, h2[t][:, 0:S], bank[:])

        out_rows = out_0.rearrange("(p t) s -> p t s", t=PACK)
        out_words = out_1[0].rearrange("p n t -> p (n t)").bitcast(I32)
        sg = sb("sg", [P, PACK, S], F32)
        sg2 = sb("sg2", [P, PACK, S], F32)
        gated = sb("gated", [P, PACK, S], F32)
        y = sb("y", [P, PACK, S], F32)
        y_bytes = sb("y_bytes", [P, S], U8)

        def first_gate(t):
            one = slice(t, t + 1)
            nc.scalar.activation(
                sg[:, t, :], h2[t][:].indirect(n3_list[:]), ACT.Sigmoid, bias=sg_bias[:, one], scale=sl_rows[:, one]
            )
            nc.vector.scalar_tensor_tensor(gated[:, t, :], sg[:, t, :], 2.0, h2[t][:, 0:S], ALU.mult, ALU.mult)

        def second_gate(t, first, last):
            one = slice(t, t + 1)
            cols = slice(first, last)
            nc.scalar.activation(
                sg2[:, t, cols], h2[t][:].indirect(entries(n4_list, first, last)), ACT.Sigmoid,
                bias=sg2_bias[:, one], scale=sg2_scale[:, one],
            )
            nc.vector.tensor_tensor(y[:, t, cols], gated[:, t, cols], sg2[:, t, cols], ALU.mult)

        for c, (first, last) in enumerate(HALVES):
            width = last - first
            for t in range(PACK):
                if c == 0:
                    first_gate(t)
                second_gate(t, first, last)
                nc.sync.dma_start(out_rows[:, t, first:last], y[:, t, first:last])
            y_grouped = sb(f"y_grouped{c}", [P, PACK * width], BF16)
            y_words = sb(f"y_words{c}", [P, width], I32)
            split = VECTOR_COLUMNS if last == S else width
            interleave(True, y_grouped[:, 0 : PACK * split], y[:, :, first : first + split])
            if split < width:
                interleave(False, y_grouped[:, PACK * split :], y[:, :, first + split : last])
            nc.vector.quantize_mx(y_words[:].bitcast(FP8X4), y_bytes[:, first:last], y_grouped[:])
            nc.sync.dma_start(out_words[:, first:last], y_words[:])
        out_bytes = out_2[0].bitcast(I32)
        for q in range(P // QUADRANT):
            queue = nc.sync if q % 2 else nc.scalar
            queue.dma_start(
                out_bytes[4 * q : 4 * q + 4, :], y_bytes[:].bitcast(I32)[QUADRANT * q : QUADRANT * q + 4, :]
            )
